import numpy as np, ml_dtypes
CORES = [8,136,40,168]
N = 4
import mx_ref
NC, G = 128, 2
C, C2 = np.float32(0.031), np.float32(0.0155)
BF = ml_dtypes.bfloat16
def cut(t, i, w=512):
    return t[:, w * i:w * i + w]
def tile(rs):
    return np.stack(rs, axis=2).reshape(128, -1).astype(BF)
def layer(w, X):
    out = []
    for i in range(G):
        for t in range(len(X)):
            p = mx_ref.matmul(mx_ref.quantize(cut(w, len(X) * i + t)), X[t])
            z = p if t == 0 else z + p
        out.append(z)
    return out
def act(Z):
    return [np.maximum(s * z, 0) * C for z in Z for s in (1, -1)]
def act2(Z):
    return [np.maximum(s * z, 0) * C2 for z in Z for s in (1, -1)]
def setup_inputs(rng):
    def f(*shape):
        return mx_ref.flush((rng.standard_normal(shape, dtype=np.float32) * np.exp2(rng.integers(-2, 3, shape[:-1] + (1,)))).astype(BF))
    return {"x": f(N, 128, 4 * NC), "w1": f(N, 128, G * 512), "w2": f(N, 128, G * 512), "w3": f(N, 128, G * 512), "w4": f(N, 128, 512)}
def setup_inputs_blocks(rng):
    d = setup_inputs(rng)
    for k in ("x", "w1", "w2", "w3", "w4"): d[k] = mx_ref.spread(d[k], rng, 2)
    return d
def setup_inputs_wide(rng):
    d = setup_inputs(rng)
    for k in ("x", "w1", "w2", "w3", "w4"): d[k] = mx_ref.flush((d[k].astype(np.float32) * np.exp2(rng.integers(-4, 5, (N, 1, 1))).astype(np.float32)).astype(BF))
    return d
def reference(x, w1, w2, w3, w4, own=None):
    X = [mx_ref.quantize(x[j]) for j in range(N)]
    t = np.stack([np.stack([tile(act(layer(w1[r], [X[c]]))) for c in range(N)]) for r in range(N)])
    uset = t if own is None else own["t"]
    h = np.zeros((N, 128, 4 * NC), BF)
    for c in range(N):
        for r in range(N):
            P = layer(w2[r], [mx_ref.quantize(uset[r][c])])
            Z = P if r == 0 else [z + p for z, p in zip(Z, P)]
        h[c] = tile(act2(Z))
    use = h if own is None else own["h"]
    H = [mx_ref.quantize(use[j]) for j in range(N)]
    y = np.zeros((N, 128, NC), np.float32)
    for c in range(N):
        for r in range(N):
            p = mx_ref.matmul(mx_ref.quantize(w4[r]), mx_ref.quantize(tile(act(layer(w3[r], [H[c]])))))
            y[c] = p if r == 0 else y[c] + p
    return {"t": t, "h": h, "y": y}

@@ -1,0 +1,281 @@
+from concourse.bass import DstId, RemoteDMATransfer
+from concourse.mybir import dt, AluOpType, ActivationFunctionType
+
+N = 4
+NC = 128
+WCOLS = 3 * 128
+NHELP = 4
+PIECE = WCOLS // NHELP
+C1, C2 = 0.031, 0.0155
+CODES = "float8_e4m3fn_x4"
+
+SCRATCH = {
+    "bx": ("sbuf", [128, 512], "bfloat16"),
+    "bw1": ("sbuf", [128, 1024], "bfloat16"),
+    "bw2": ("sbuf", [128, 1024], "bfloat16"),
+    "bw3": ("sbuf", [128, 1024], "bfloat16"),
+    "bw4": ("sbuf", [128, 512], "bfloat16"),
+    "qx": ("sbuf", [128, N * NC], CODES),
+    "sx": ("sbuf", [128, N * NC], "uint8"),
+    "qw1": ("sbuf", [128, 256], CODES),
+    "sw1": ("sbuf", [128, 256], "uint8"),
+    "qw2": ("sbuf", [128, 256], CODES),
+    "sw2": ("sbuf", [128, 256], "uint8"),
+    "qw": ("sbuf", [128, N * WCOLS], CODES),
+    "sw": ("sbuf", [128, N * WCOLS], "uint8"),
+    "rq": ("sbuf", [128, PIECE], CODES),
+    "rs": ("sbuf", [128, PIECE], "uint8"),
+    "tt": ("sbuf", [128, N * 512], "bfloat16"),
+    "qt": ("sbuf", [128, N * NC], CODES),
+    "st": ("sbuf", [128, N * NC], "uint8"),
+    "part": ("sbuf", [128, N * 256], "float32"),
+    "land": ("sbuf", [128, N * NC], "float32"),
+    "fold": ("sbuf", [128, 256], "float32"),
+    "sums": ("sbuf", [128, 256], "float32"),
+    "hh": ("sbuf", [128, 512], "bfloat16"),
+    "qh": ("sbuf", [128, NC], CODES),
+    "sh": ("sbuf", [128, NC], "uint8"),
+    "uu": ("sbuf", [128, N * 512], "bfloat16"),
+    "qu": ("sbuf", [128, N * NC], CODES),
+    "su": ("sbuf", [128, N * NC], "uint8"),
+    "yy": ("sbuf", [128, NC], "float32"),
+    "ps": ("psum", [128, 4096], "float32"),
+}
+SEMAPHORES = (["lx", "lw1", "lw2", "lw3", "lw4", "qdx", "qdw", "qd1", "qd2", "stored",
+               "wc", "wp", "warr", "sarr", "f0", "f1", "left", "sleft",
+               "h0", "h1", "ha", "hq", "ydone", "yc"]
+              + ["x%d" % k for k in range(N)]
+              + [s + str(k) for k in range(N) for s in ("za", "zb", "act", "tq", "pa", "pb", "out", "va", "vb", "uact", "uq")])
+
+
+def engines(mask):
+    return [e for e in range(mask.bit_length()) if mask >> e & 1]
+
+
+def mask_of(es):
+    return sum(1 << e for e in es)
+
+
+def chip_of(c, topo):
+    return topo.host(c), topo.chip(c)
+
+
+def helpers_of(rc, topo):
+    mine = [d for d in range(256) if d != rc and chip_of(d, topo) == chip_of(rc, topo)]
+    near = [d for d in mine if topo.die(d) == topo.die(rc)]
+    far = [d for d in mine if topo.die(d) != topo.die(rc)]
+    return near[:2] + far[:2]
+
+
+def dest(dst, src, topo):
+    rid, pid = topo.addr(dst, src)
+    return DstId(rid=rid, pnc=pid)
+
+
+def rank_program(g, core, T, topo):
+    rank = T.rank_of(core)
+    if rank is not None:
+        rank_core(g, core, rank, T, topo)
+        return
+    for r in range(N):
+        if core in helpers_of(T.cores[r], topo):
+            helper_core(g, core, r, helpers_of(T.cores[r], topo).index(core), T, topo)
+
+
+def helper_core(g, core, r, k, T, topo):
+    S = T.sem
+    others = [T.cores[(r + j) % N] for j in range(1, N)]
+    off = engines(topo.mask(core, others[0]))
+    a = r * WCOLS + k * PIECE
+    ids = [dest(d, core, topo) for d in others]
+    g.wait_ge(S["wc"], 2)
+    g.remote_dma_fused([RemoteDMATransfer(
+        dst_ids=ids, dma_engine_mask=mask_of(off), remote_sem=S["warr"],
+        srcs=[T["rq"][:, 0:PIECE].bitcast(dt.uint8)],
+        dsts=[T["qw"][:, a:a + PIECE].bitcast(dt.uint8) for _ in others])], local_sem=S["left"])
+    g.wait_ge(S["wp"], 2)
+    g.remote_dma_fused([RemoteDMATransfer(
+        dst_ids=ids, dma_engine_mask=mask_of(off), remote_sem=S["warr"],
+        srcs=[T["rs"][:, 0:PIECE]],
+        dsts=[T["sw"][:, a:a + PIECE] for _ in others])], local_sem=S["left"])
+    n = 2 * len(off)
+    if k < 2:
+        slots = [(r + j) % N for j in range(1, N)]
+        g.wait_ge(S["sarr"], 3 * (len(off) // 2))
+        g.remote_dma_fused([RemoteDMATransfer(
+            dst_ids=[dest(T.cores[r], core, topo)], dma_engine_mask=mask_of(off), remote_sem=S["f%d" % k],
+            srcs=[T["land"][:, s * NC:s * NC + NC] for s in slots],
+            dsts=[T["fold"][:, k * NC:k * NC + NC]], alu_op=1)], local_sem=S["left"])
+        n += len(off)
+    g.wait_ge(S["left"], n)
+
+
+def rank_core(g, core, rank, T, topo):
+    S = T.sem
+    order = [(rank + k) % N for k in range(N)]
+    others = [T.cores[c] for c in order[1:]]
+    helpers = helpers_of(core, topo)
+    off = engines(topo.mask(core, others[0]))
+    chip_only = [e for e in engines(topo.mask(core, helpers[0])) if e not in off]
+    relu, copy = ActivationFunctionType.Relu, ActivationFunctionType.Copy
+
+    def bank(b):
+        return T["ps"][:, 512 * b:512 * b + NC]
+
+    def cols(name, i, w=NC):
+        return T[name][:, i * w:i * w + w]
+
+    for name in ("x", "w3", "w4"):
+        g.sync.dma_start(T["b" + name][:], T[name][:]).then_inc(S["l" + name], 16)
+    g.scalar.wait_ge(S["lx"], 16)
+    for name in ("w1", "w2"):
+        g.scalar.dma_start(T["b" + name][:], T[name][:]).then_inc(S["l" + name], 16)
+
+    def relus(eng, src, buf, slot, i, c, sem):
+        for s in (0, 1):
+            out = T[buf][:, 512 * slot + 2 * i + s:512 * slot + 512:4]
+            f = -c if s else c
+            if eng == "scalar":
+                g.scalar.activation(out, src, relu, scale=f).then_inc(S[sem], 1)
+            else:
+                g.vector.tensor_scalar(out, src, f, 0.0, AluOpType.mult, AluOpType.max).then_inc(S[sem], 1)
+
+    def mm(b, w, sw, wi, m, sm, mi, start=True, stop=True):
+        return g.tensor.matmul_mx(bank(b), cols(w, wi), cols(sw, wi), cols(m, mi), cols(sm, mi), start, stop)
+
+    def z_mm(k):
+        mm(2 * k, "qw1", "sw1", 0, "qx", "sx", order[k]).then_inc(S["za%d" % k], 1)
+        mm(2 * k + 1, "qw1", "sw1", 1, "qx", "sx", order[k]).then_inc(S["zb%d" % k], 1)
+
+    def p_mm(k):
+        g.tensor.wait_ge(S["tq%d" % k], 1)
+        mm(2 * k, "qw2", "sw2", 0, "qt", "st", order[k]).then_inc(S["pa%d" % k], 1)
+        mm(2 * k + 1, "qw2", "sw2", 1, "qt", "st", order[k]).then_inc(S["pb%d" % k], 1)
+
+    def t_scalar(k):
+        g.scalar.wait_ge(S["za%d" % k], 1)
+        relus("scalar", bank(2 * k), "tt", order[k], 0, C1, "act%d" % k)
+
+    def t_vector(k):
+        g.vector.wait_ge(S["zb%d" % k], 1)
+        relus("vector", bank(2 * k + 1), "tt", order[k], 1, C1, "act%d" % k)
+        g.vector.wait_ge(S["act%d" % k], 4)
+        g.vector.quantize_mx(cols("qt", order[k]), cols("st", order[k]), cols("tt", order[k], 512)).then_inc(S["tq%d" % k], 1)
+
+    def p_scalar(k):
+        g.scalar.wait_ge(S["pa%d" % k], 1)
+        g.scalar.activation(cols("part", 2 * k), bank(2 * k), copy).then_inc(S["out%d" % k], 1)
+
+    def p_vector(k):
+        g.vector.wait_ge(S["pb%d" % k], 1)
+        g.vector.tensor_copy(cols("part", 2 * k + 1), bank(2 * k + 1)).then_inc(S["out%d" % k], 1)
+
+    g.vector.wait_ge(S["lx"], 16)
+    g.vector.quantize_mx(cols("qx", rank), cols("sx", rank), T["bx"][:, 0:512]).then_inc(S["qdx"], 1)
+    for name, i, j in (("w3", 0, 0), ("w3", 1, 1), ("w4", 0, 2)):
+        if i == 0:
+            g.vector.wait_ge(S["l" + name], 16)
+        g.vector.quantize_mx(cols("qw", 3 * rank + j), cols("sw", 3 * rank + j), cols("b" + name, i, 512)).then_inc(S["qdw"], 1)
+    for name in ("1", "2"):
+        g.vector.wait_ge(S["lw" + name], 16)
+        for i in (0, 1):
+            g.vector.quantize_mx(cols("qw" + name, i), cols("sw" + name, i), cols("bw" + name, i, 512)).then_inc(S["qd" + name], 1)
+
+    ids = [dest(d, core, topo) for d in others]
+    a = rank * NC
+    g.wait_ge(S["qdx"], 1)
+    g.remote_dma_fused([RemoteDMATransfer(
+        dst_ids=ids, dma_engine_mask=mask_of(off), remote_sem=S["x%d" % rank],
+        srcs=[T["qx"][:, a:a + NC].bitcast(dt.uint8)],
+        dsts=[T["qx"][:, a:a + NC].bitcast(dt.uint8) for _ in others])], local_sem=S["left"])
+    g.remote_dma_fused([RemoteDMATransfer(
+        dst_ids=ids, dma_engine_mask=mask_of(off), remote_sem=S["x%d" % rank],
+        srcs=[T["sx"][:, a:a + NC]], dsts=[T["sx"][:, a:a + NC] for _ in others])], local_sem=S["left"])
+    g.wait_ge(S["qdw"], 3)
+    per = len(chip_only) // NHELP
+    for code in (True, False):
+        trs = []
+        for k, d in enumerate(helpers):
+            b = rank * WCOLS + k * PIECE
+            src = T["qw"][:, b:b + PIECE].bitcast(dt.uint8) if code else T["sw"][:, b:b + PIECE]
+            dst = T["rq"][:, 0:PIECE].bitcast(dt.uint8) if code else T["rs"][:, 0:PIECE]
+            trs.append(RemoteDMATransfer(
+                dst_ids=[dest(d, core, topo)], dma_engine_mask=mask_of(chip_only[per * k:per * k + per]),
+                remote_sem=S["wc" if code else "wp"], srcs=[src], dsts=[dst]))
+        g.remote_dma_fused(trs, local_sem=S["left"])
+    half = len(off) // 2
+    for k in (1, 2, 3):
+        near = helpers_of(T.cores[order[k]], topo)[:2]
+        g.wait_ge(S["out%d" % k], 2)
+        g.remote_dma_fused([RemoteDMATransfer(
+            dst_ids=[dest(near[i], core, topo)], dma_engine_mask=mask_of(off[half * i:half * i + half]), remote_sem=S["sarr"],
+            srcs=[cols("part", 2 * k + i)], dsts=[cols("land", rank)]) for i in (0, 1)], local_sem=S["sleft"])
+    g.wait_ge(S["left"], 2 * len(off) + 2 * per * NHELP)
+
+    g.tensor.wait_ge(S["qd1"], 2)
+    g.tensor.wait_ge(S["qdx"], 1)
+    z_mm(0)
+    g.tensor.wait_ge(S["qd2"], 2)
+    p_mm(0)
+    xs = 2 * len(off)
+    for k in (1, 2):
+        g.tensor.wait_ge(S["x%d" % order[k]], xs)
+        z_mm(k)
+    p_mm(1)
+    g.tensor.wait_ge(S["x%d" % order[3]], xs)
+    z_mm(3)
+    p_mm(2)
+    p_mm(3)
+    for k in (0, 1, 2):
+        t_scalar(k)
+        t_vector(k)
+    p_scalar(1)
+    p_vector(1)
+    t_scalar(3)
+    t_vector(3)
+    for k in (2, 3):
+        p_scalar(k)
+        p_vector(k)
+
+    for i in (0, 1):
+        g.vector.wait_ge(S["f%d" % i], len(off))
+        if i == 0:
+            g.vector.wait_ge(S["pa0"], 1)
+            g.vector.wait_ge(S["pb0"], 1)
+        g.vector.tensor_tensor(cols("sums", i), bank(i), cols("fold", i), AluOpType.add).then_inc(S["h%d" % i], 1)
+    g.scalar.wait_ge(S["h0"], 1)
+    relus("scalar", cols("sums", 0), "hh", 0, 0, C2, "ha")
+    g.vector.wait_ge(S["h1"], 1)
+    relus("vector", cols("sums", 1), "hh", 0, 1, C2, "ha")
+    g.vector.wait_ge(S["ha"], 4)
+    g.vector.quantize_mx(cols("qh", 0), cols("sh", 0), T["hh"][:, 0:512]).then_inc(S["hq"], 1)
+
+    g.tensor.wait_ge(S["hq"], 1)
+    for k in range(N):
+        r = order[k]
+        if k == 1:
+            g.tensor.wait_ge(S["warr"], 3 * NHELP * xs)
+        mm(2 * k, "qw", "sw", 3 * r, "qh", "sh", 0).then_inc(S["va%d" % k], 1)
+        mm(2 * k + 1, "qw", "sw", 3 * r + 1, "qh", "sh", 0).then_inc(S["vb%d" % k], 1)
+    for k in range(N):
+        g.scalar.wait_ge(S["va%d" % k], 1)
+        relus("scalar", bank(2 * k), "uu", k, 0, C1, "uact%d" % k)
+        g.vector.wait_ge(S["vb%d" % k], 1)
+        relus("vector", bank(2 * k + 1), "uu", k, 1, C1, "uact%d" % k)
+        g.vector.wait_ge(S["uact%d" % k], 4)
+        g.vector.quantize_mx(cols("qu", k), cols("su", k), cols("uu", k, 512)).then_inc(S["uq%d" % k], 1)
+        g.tensor.wait_ge(S["uq%d" % k], 1)
+        p = mm(0, "qw", "sw", 3 * order[k] + 2, "qu", "su", k, start=k == 0, stop=k == N - 1)
+    p.then_inc(S["ydone"], 1)
+    g.vector.wait_ge(S["ydone"], 1)
+    g.vector.tensor_copy(cols("yy", 0), bank(0)).then_inc(S["yc"], 1)
+
+    g.sync.wait_ge(S["sleft"], 3 * len(off))
+    for k in range(N):
+        g.sync.wait_ge(S["act%d" % k], 4)
+        g.sync.dma_start(T["t"][order[k]], cols("tt", order[k], 512)).then_inc(S["stored"], 16)
+    g.sync.wait_ge(S["ha"], 4)
+    g.sync.dma_start(T["h"][:], T["hh"][:]).then_inc(S["stored"], 16)
+    g.sync.wait_ge(S["yc"], 1)
+    g.sync.dma_start(T["y"][:], T["yy"][:]).then_inc(S["stored"], 16)
+    g.sync.wait_ge(S["stored"], 16 * (N + 2))

@@ -4,8 +4,8 @@ from concourse.mybir import dt, AluOpType, ActivationFunctionType
 N = 4
 NC = 128
 WCOLS = 3 * 128
-NHELP = 4
-PIECE = WCOLS // NHELP
+NNEAR, NFAR = 2, 4
+FARW, NEARW = WCOLS // NFAR, WCOLS // NNEAR
 C1, C2 = 0.031, 0.0155
 CODES = "float8_e4m3fn_x4"
 
@@ -23,13 +23,15 @@ SCRATCH = {
     "sw2": ("sbuf", [128, 256], "uint8"),
     "qw": ("sbuf", [128, N * WCOLS], CODES),
     "sw": ("sbuf", [128, N * WCOLS], "uint8"),
-    "rq": ("sbuf", [128, PIECE], CODES),
-    "rs": ("sbuf", [128, PIECE], "uint8"),
+    "rq": ("sbuf", [128, FARW], CODES),
+    "rs": ("sbuf", [128, NEARW], "uint8"),
     "tt": ("sbuf", [128, N * 512], "bfloat16"),
     "qt": ("sbuf", [128, N * NC], CODES),
     "st": ("sbuf", [128, N * NC], "uint8"),
     "part": ("sbuf", [128, N * 256], "float32"),
     "land": ("sbuf", [128, N * NC], "float32"),
+    "two": ("sbuf", [128, NC], "float32"),
+    "three": ("sbuf", [128, NC], "float32"),
     "fold": ("sbuf", [128, 256], "float32"),
     "sums": ("sbuf", [128, 256], "float32"),
     "hh": ("sbuf", [128, 512], "bfloat16"),
@@ -42,7 +44,7 @@ SCRATCH = {
     "ps": ("psum", [128, 4096], "float32"),
 }
 SEMAPHORES = (["lx", "lw1", "lw2", "lw3", "lw4", "qdx", "qdw", "qd1", "qd2", "stored",
-               "wc", "wp", "warr", "sarr", "f0", "f1", "left", "sleft",
+               "wgot", "warr", "sa1", "sa2", "sa3", "hv2", "hv3", "f0", "f1", "left", "sleft",
                "h0", "h1", "ha", "hq", "ydone", "yc"]
               + ["x%d" % k for k in range(N)]
               + [s + str(k) for k in range(N) for s in ("za", "zb", "act", "tq", "pa", "pb", "out", "va", "vb", "uact", "uq")])
@@ -64,7 +66,7 @@ def helpers_of(rc, topo):
     mine = [d for d in range(256) if d != rc and chip_of(d, topo) == chip_of(rc, topo)]
     near = [d for d in mine if topo.die(d) == topo.die(rc)]
     far = [d for d in mine if topo.die(d) != topo.die(rc)]
-    return near[:2] + far[:2]
+    return near[:NNEAR], far[:NFAR]
 
 
 def dest(dst, src, topo):
@@ -78,45 +80,56 @@ def rank_program(g, core, T, topo):
         rank_core(g, core, rank, T, topo)
         return
     for r in range(N):
-        if core in helpers_of(T.cores[r], topo):
-            helper_core(g, core, r, helpers_of(T.cores[r], topo).index(core), T, topo)
+        near, far = helpers_of(T.cores[r], topo)
+        if core in near:
+            near_core(g, core, r, near.index(core), T, topo)
+        if core in far:
+            far_core(g, core, r, far.index(core), T, topo)
 
 
-def helper_core(g, core, r, k, T, topo):
+def far_core(g, core, r, k, T, topo):
     S = T.sem
     others = [T.cores[(r + j) % N] for j in range(1, N)]
     off = engines(topo.mask(core, others[0]))
-    a = r * WCOLS + k * PIECE
-    ids = [dest(d, core, topo) for d in others]
-    g.wait_ge(S["wc"], 2)
+    a = r * WCOLS + k * FARW
+    g.wait_ge(S["wgot"], 2)
     g.remote_dma_fused([RemoteDMATransfer(
-        dst_ids=ids, dma_engine_mask=mask_of(off), remote_sem=S["warr"],
-        srcs=[T["rq"][:, 0:PIECE].bitcast(dt.uint8)],
-        dsts=[T["qw"][:, a:a + PIECE].bitcast(dt.uint8) for _ in others])], local_sem=S["left"])
-    g.wait_ge(S["wp"], 2)
+        dst_ids=[dest(d, core, topo) for d in others], dma_engine_mask=mask_of(off), remote_sem=S["warr"],
+        srcs=[T["rq"][:, 0:FARW].bitcast(dt.uint8)],
+        dsts=[T["qw"][:, a:a + FARW].bitcast(dt.uint8) for _ in others])], local_sem=S["left"])
+    g.wait_ge(S["left"], len(off))
+
+
+def near_core(g, core, r, k, T, topo):
+    S = T.sem
+    others = [T.cores[(r + j) % N] for j in range(1, N)]
+    off = engines(topo.mask(core, others[0]))
+    a = r * WCOLS + k * NEARW
+    g.wait_ge(S["wgot"], 4)
     g.remote_dma_fused([RemoteDMATransfer(
-        dst_ids=ids, dma_engine_mask=mask_of(off), remote_sem=S["warr"],
-        srcs=[T["rs"][:, 0:PIECE]],
-        dsts=[T["sw"][:, a:a + PIECE] for _ in others])], local_sem=S["left"])
-    n = 2 * len(off)
-    if k < 2:
-        slots = [(r + j) % N for j in range(1, N)]
-        g.wait_ge(S["sarr"], 3 * (len(off) // 2))
-        g.remote_dma_fused([RemoteDMATransfer(
-            dst_ids=[dest(T.cores[r], core, topo)], dma_engine_mask=mask_of(off), remote_sem=S["f%d" % k],
-            srcs=[T["land"][:, s * NC:s * NC + NC] for s in slots],
-            dsts=[T["fold"][:, k * NC:k * NC + NC]], alu_op=1)], local_sem=S["left"])
-        n += len(off)
-    g.wait_ge(S["left"], n)
+        dst_ids=[dest(d, core, topo) for d in others], dma_engine_mask=mask_of(off), remote_sem=S["warr"],
+        srcs=[T["rs"][:, 0:NEARW]],
+        dsts=[T["sw"][:, a:a + NEARW] for _ in others])], local_sem=S["left"])
+    land = [T["land"][:, ((r - j) % N) * NC:((r - j) % N) * NC + NC] for j in range(N)]
+    for j in (1, 2):
+        g.vector.wait_ge(S["sa%d" % j], len(off) // 2)
+    g.vector.tensor_tensor(T["two"][:, 0:NC], land[1], land[2], AluOpType.add).then_inc(S["hv2"], 1)
+    g.vector.wait_ge(S["hv2"], 1)
+    g.vector.wait_ge(S["sa3"], len(off) // 2)
+    g.vector.tensor_tensor(T["three"][:, 0:NC], T["two"][:, 0:NC], land[3], AluOpType.add).then_inc(S["hv3"], 1)
+    rid, pid = topo.addr(T.cores[r], core)
+    g.wait_ge(S["hv3"], 1)
+    g.remote_dma(T["fold"][:, k * NC:k * NC + NC], T["three"][:, 0:NC], S["f%d" % k], S["left"], pid, rid, mask_of(off))
+    g.wait_ge(S["left"], 2 * len(off))
 
 
 def rank_core(g, core, rank, T, topo):
     S = T.sem
     order = [(rank + k) % N for k in range(N)]
     others = [T.cores[c] for c in order[1:]]
-    helpers = helpers_of(core, topo)
+    near, far = helpers_of(core, topo)
     off = engines(topo.mask(core, others[0]))
-    chip_only = [e for e in engines(topo.mask(core, helpers[0])) if e not in off]
+    chip_only = [e for e in engines(topo.mask(core, near[0])) if e not in off]
     relu, copy = ActivationFunctionType.Relu, ActivationFunctionType.Copy
 
     def bank(b):
@@ -192,25 +205,23 @@ def rank_core(g, core, rank, T, topo):
         dst_ids=ids, dma_engine_mask=mask_of(off), remote_sem=S["x%d" % rank],
         srcs=[T["sx"][:, a:a + NC]], dsts=[T["sx"][:, a:a + NC] for _ in others])], local_sem=S["left"])
     g.wait_ge(S["qdw"], 3)
-    per = len(chip_only) // NHELP
-    for code in (True, False):
-        trs = []
-        for k, d in enumerate(helpers):
-            b = rank * WCOLS + k * PIECE
-            src = T["qw"][:, b:b + PIECE].bitcast(dt.uint8) if code else T["sw"][:, b:b + PIECE]
-            dst = T["rq"][:, 0:PIECE].bitcast(dt.uint8) if code else T["rs"][:, 0:PIECE]
-            trs.append(RemoteDMATransfer(
-                dst_ids=[dest(d, core, topo)], dma_engine_mask=mask_of(chip_only[per * k:per * k + per]),
-                remote_sem=S["wc" if code else "wp"], srcs=[src], dsts=[dst]))
-        g.remote_dma_fused(trs, local_sem=S["left"])
+    b = rank * WCOLS
+    g.remote_dma_fused([RemoteDMATransfer(
+        dst_ids=[dest(d, core, topo)], dma_engine_mask=mask_of(chip_only[2 * k:2 * k + 2]), remote_sem=S["wgot"],
+        srcs=[T["qw"][:, b + k * FARW:b + k * FARW + FARW].bitcast(dt.uint8)],
+        dsts=[T["rq"][:, 0:FARW].bitcast(dt.uint8)]) for k, d in enumerate(far)], local_sem=S["left"])
+    g.remote_dma_fused([RemoteDMATransfer(
+        dst_ids=[dest(d, core, topo)], dma_engine_mask=mask_of(chip_only[4 * k:4 * k + 4]), remote_sem=S["wgot"],
+        srcs=[T["sw"][:, b + k * NEARW:b + k * NEARW + NEARW]],
+        dsts=[T["rs"][:, 0:NEARW]]) for k, d in enumerate(near)], local_sem=S["left"])
     half = len(off) // 2
     for k in (1, 2, 3):
-        near = helpers_of(T.cores[order[k]], topo)[:2]
+        theirs = helpers_of(T.cores[order[k]], topo)[0]
         g.wait_ge(S["out%d" % k], 2)
         g.remote_dma_fused([RemoteDMATransfer(
-            dst_ids=[dest(near[i], core, topo)], dma_engine_mask=mask_of(off[half * i:half * i + half]), remote_sem=S["sarr"],
+            dst_ids=[dest(theirs[i], core, topo)], dma_engine_mask=mask_of(off[half * i:half * i + half]), remote_sem=S["sa%d" % k],
             srcs=[cols("part", 2 * k + i)], dsts=[cols("land", rank)]) for i in (0, 1)], local_sem=S["sleft"])
-    g.wait_ge(S["left"], 2 * len(off) + 2 * per * NHELP)
+    g.wait_ge(S["left"], 2 * len(off) + 2 * NFAR + 4 * NNEAR)
 
     g.tensor.wait_ge(S["qd1"], 2)
     g.tensor.wait_ge(S["qdx"], 1)
@@ -238,10 +249,10 @@ def rank_core(g, core, rank, T, topo):
         p_vector(k)
 
     for i in (0, 1):
-        g.vector.wait_ge(S["f%d" % i], len(off))
         if i == 0:
             g.vector.wait_ge(S["pa0"], 1)
             g.vector.wait_ge(S["pb0"], 1)
+        g.vector.wait_ge(S["f%d" % i], len(off))
         g.vector.tensor_tensor(cols("sums", i), bank(i), cols("fold", i), AluOpType.add).then_inc(S["h%d" % i], 1)
     g.scalar.wait_ge(S["h0"], 1)
     relus("scalar", cols("sums", 0), "hh", 0, 0, C2, "ha")
@@ -252,18 +263,21 @@ def rank_core(g, core, rank, T, topo):
 
     g.tensor.wait_ge(S["hq"], 1)
     for k in range(N):
-        r = order[k]
         if k == 1:
-            g.tensor.wait_ge(S["warr"], 3 * NHELP * xs)
-        mm(2 * k, "qw", "sw", 3 * r, "qh", "sh", 0).then_inc(S["va%d" % k], 1)
-        mm(2 * k + 1, "qw", "sw", 3 * r + 1, "qh", "sh", 0).then_inc(S["vb%d" % k], 1)
+            g.tensor.wait_ge(S["warr"], 3 * (NNEAR + NFAR) * len(off))
+        mm(2 * k, "qw", "sw", 3 * order[k], "qh", "sh", 0).then_inc(S["va%d" % k], 1)
+        mm(2 * k + 1, "qw", "sw", 3 * order[k] + 1, "qh", "sh", 0).then_inc(S["vb%d" % k], 1)
     for k in range(N):
         g.scalar.wait_ge(S["va%d" % k], 1)
         relus("scalar", bank(2 * k), "uu", k, 0, C1, "uact%d" % k)
-        g.vector.wait_ge(S["vb%d" % k], 1)
-        relus("vector", bank(2 * k + 1), "uu", k, 1, C1, "uact%d" % k)
-        g.vector.wait_ge(S["uact%d" % k], 4)
-        g.vector.quantize_mx(cols("qu", k), cols("su", k), cols("uu", k, 512)).then_inc(S["uq%d" % k], 1)
+    for k in range(N + 1):
+        if k < N:
+            g.vector.wait_ge(S["vb%d" % k], 1)
+            relus("vector", bank(2 * k + 1), "uu", k, 1, C1, "uact%d" % k)
+        if k > 0:
+            g.vector.wait_ge(S["uact%d" % (k - 1)], 4)
+            g.vector.quantize_mx(cols("qu", k - 1), cols("su", k - 1), cols("uu", k - 1, 512)).then_inc(S["uq%d" % (k - 1)], 1)
+    for k in range(N):
         g.tensor.wait_ge(S["uq%d" % k], 1)
         p = mm(0, "qw", "sw", 3 * order[k] + 2, "qu", "su", k, start=k == 0, stop=k == N - 1)
     p.then_inc(S["ydone"], 1)

@@ -6,6 +6,8 @@ NC = 128
 WCOLS = 3 * 128
 NNEAR, NFAR = 2, 4
 FARW, NEARW = WCOLS // NFAR, WCOLS // NNEAR
+STRAIGHT = 200
+CUT = STRAIGHT - NC
 C1, C2 = 0.031, 0.0155
 CODES = "float8_e4m3fn_x4"
 
@@ -31,8 +33,10 @@ SCRATCH = {
     "part": ("sbuf", [128, N * 256], "float32"),
     "land": ("sbuf", [128, N * NC], "float32"),
     "two": ("sbuf", [128, NC], "float32"),
-    "three": ("sbuf", [128, NC], "float32"),
+    "three": ("sbuf", [128, NC - CUT], "float32"),
+    "straight": ("sbuf", [128, STRAIGHT], "float32"),
     "fold": ("sbuf", [128, 256], "float32"),
+    "pre": ("sbuf", [128, STRAIGHT], "float32"),
     "sums": ("sbuf", [128, 256], "float32"),
     "hh": ("sbuf", [128, 512], "bfloat16"),
     "qh": ("sbuf", [128, NC], CODES),
@@ -43,9 +47,9 @@ SCRATCH = {
     "yy": ("sbuf", [128, NC], "float32"),
     "ps": ("psum", [128, 4096], "float32"),
 }
-SEMAPHORES = (["lx", "lw1", "lw2", "lw3", "lw4", "qdx", "qdw", "qd1", "qd2", "stored",
-               "wgot", "warr", "sa1", "sa2", "sa3", "hv2", "hv3", "f0", "f1", "left", "sleft",
-               "h0", "h1", "ha", "hq", "ydone", "yc"]
+SEMAPHORES = (["xissued", "lx", "lw1", "lw2", "lw3", "lw4", "qdx", "qdw", "qd1", "qd2", "stored",
+               "wgot", "warr", "sa1", "sa2", "sa3", "hv2", "hv3", "f0", "f1", "f2", "sstr", "left", "sleft",
+               "pre0", "h0", "h1", "ha", "hq", "ydone", "yc"]
               + ["x%d" % k for k in range(N)]
               + [s + str(k) for k in range(N) for s in ("za", "zb", "act", "tq", "pa", "pb", "out", "va", "vb", "uact", "uq")])
 
@@ -110,39 +114,52 @@ def near_core(g, core, r, k, T, topo):
         dst_ids=[dest(d, core, topo) for d in others], dma_engine_mask=mask_of(off), remote_sem=S["warr"],
         srcs=[T["rs"][:, 0:NEARW]],
         dsts=[T["sw"][:, a:a + NEARW] for _ in others])], local_sem=S["left"])
-    land = [T["land"][:, ((r - j) % N) * NC:((r - j) % N) * NC + NC] for j in range(N)]
+
+    def land(j, lo):
+        return T["land"][:, j * NC + lo:j * NC + NC]
+
     for j in (1, 2):
         g.vector.wait_ge(S["sa%d" % j], len(off) // 2)
-    g.vector.tensor_tensor(T["two"][:, 0:NC], land[1], land[2], AluOpType.add).then_inc(S["hv2"], 1)
-    g.vector.wait_ge(S["hv2"], 1)
-    g.vector.wait_ge(S["sa3"], len(off) // 2)
-    g.vector.tensor_tensor(T["three"][:, 0:NC], T["two"][:, 0:NC], land[3], AluOpType.add).then_inc(S["hv3"], 1)
+    g.vector.tensor_tensor(T["two"][:, 0:NC], land(1, 0), land(2, 0), AluOpType.add).then_inc(S["hv2"], 1)
     rid, pid = topo.addr(T.cores[r], core)
-    g.wait_ge(S["hv3"], 1)
-    g.remote_dma(T["fold"][:, k * NC:k * NC + NC], T["three"][:, 0:NC], S["f%d" % k], S["left"], pid, rid, mask_of(off))
-    g.wait_ge(S["left"], 2 * len(off))
+    w = CUT if k else NC
+    g.wait_ge(S["hv2"], 1)
+    g.remote_dma(T["fold"][:, k * NC:k * NC + w], T["two"][:, 0:w], S["f%d" % k], S["left"], pid, rid, mask_of(off))
+    n = 2 * len(off)
+    if k:
+        g.vector.wait_ge(S["hv2"], 1)
+        g.vector.wait_ge(S["sa3"], len(off))
+        g.vector.tensor_tensor(T["three"][:, 0:NC - CUT], T["two"][:, CUT:NC], land(3, CUT), AluOpType.add).then_inc(S["hv3"], 1)
+        g.wait_ge(S["hv3"], 1)
+        g.remote_dma(T["fold"][:, STRAIGHT:256], T["three"][:, 0:NC - CUT], S["f2"], S["left"], pid, rid, mask_of(off))
+        n += len(off)
+    g.wait_ge(S["left"], n)
 
 
 def rank_core(g, core, rank, T, topo):
     S = T.sem
     order = [(rank + k) % N for k in range(N)]
-    others = [T.cores[c] for c in order[1:]]
     near, far = helpers_of(core, topo)
-    off = engines(topo.mask(core, others[0]))
+    off = engines(topo.mask(core, T.cores[order[1]]))
     chip_only = [e for e in engines(topo.mask(core, near[0])) if e not in off]
     relu, copy = ActivationFunctionType.Relu, ActivationFunctionType.Copy
 
-    def bank(b):
-        return T["ps"][:, 512 * b:512 * b + NC]
+    def bank(b, lo=0, hi=NC):
+        return T["ps"][:, 512 * b + lo:512 * b + hi]
 
     def cols(name, i, w=NC):
         return T[name][:, i * w:i * w + w]
 
-    for name in ("x", "w3", "w4"):
-        g.sync.dma_start(T["b" + name][:], T[name][:]).then_inc(S["l" + name], 16)
-    g.scalar.wait_ge(S["lx"], 16)
-    for name in ("w1", "w2"):
-        g.scalar.dma_start(T["b" + name][:], T[name][:]).then_inc(S["l" + name], 16)
+    def load(q, name):
+        q.dma_start(T["b" + name][:], T[name][:]).then_inc(S["l" + name], 16)
+
+    load(g.sync, "x")
+    g.sync.sem_inc(S["xissued"], 1)
+    load(g.sync, "w3")
+    load(g.sync, "w4")
+    g.scalar.wait_ge(S["xissued"], 1)
+    load(g.scalar, "w1")
+    load(g.scalar, "w2")
 
     def relus(eng, src, buf, slot, i, c, sem):
         for s in (0, 1):
@@ -157,6 +174,8 @@ def rank_core(g, core, rank, T, topo):
         return g.tensor.matmul_mx(bank(b), cols(w, wi), cols(sw, wi), cols(m, mi), cols(sm, mi), start, stop)
 
     def z_mm(k):
+        if k > 0:
+            g.tensor.wait_ge(S["x%d" % order[k]], 2 * len(off))
         mm(2 * k, "qw1", "sw1", 0, "qx", "sx", order[k]).then_inc(S["za%d" % k], 1)
         mm(2 * k + 1, "qw1", "sw1", 1, "qx", "sx", order[k]).then_inc(S["zb%d" % k], 1)
 
@@ -165,23 +184,22 @@ def rank_core(g, core, rank, T, topo):
         mm(2 * k, "qw2", "sw2", 0, "qt", "st", order[k]).then_inc(S["pa%d" % k], 1)
         mm(2 * k + 1, "qw2", "sw2", 1, "qt", "st", order[k]).then_inc(S["pb%d" % k], 1)
 
-    def t_scalar(k):
+    def make_t(k):
         g.scalar.wait_ge(S["za%d" % k], 1)
         relus("scalar", bank(2 * k), "tt", order[k], 0, C1, "act%d" % k)
-
-    def t_vector(k):
         g.vector.wait_ge(S["zb%d" % k], 1)
         relus("vector", bank(2 * k + 1), "tt", order[k], 1, C1, "act%d" % k)
         g.vector.wait_ge(S["act%d" % k], 4)
         g.vector.quantize_mx(cols("qt", order[k]), cols("st", order[k]), cols("tt", order[k], 512)).then_inc(S["tq%d" % k], 1)
 
-    def p_scalar(k):
+    def take_p(k):
         g.scalar.wait_ge(S["pa%d" % k], 1)
         g.scalar.activation(cols("part", 2 * k), bank(2 * k), copy).then_inc(S["out%d" % k], 1)
-
-    def p_vector(k):
         g.vector.wait_ge(S["pb%d" % k], 1)
         g.vector.tensor_copy(cols("part", 2 * k + 1), bank(2 * k + 1)).then_inc(S["out%d" % k], 1)
+
+    def add(out, a, b, sem):
+        g.vector.tensor_tensor(out, a, b, AluOpType.add).then_inc(S[sem], 1)
 
     g.vector.wait_ge(S["lx"], 16)
     g.vector.quantize_mx(cols("qx", rank), cols("sx", rank), T["bx"][:, 0:512]).then_inc(S["qdx"], 1)
@@ -194,16 +212,16 @@ def rank_core(g, core, rank, T, topo):
         for i in (0, 1):
             g.vector.quantize_mx(cols("qw" + name, i), cols("sw" + name, i), cols("bw" + name, i, 512)).then_inc(S["qd" + name], 1)
 
-    ids = [dest(d, core, topo) for d in others]
-    a = rank * NC
     g.wait_ge(S["qdx"], 1)
-    g.remote_dma_fused([RemoteDMATransfer(
-        dst_ids=ids, dma_engine_mask=mask_of(off), remote_sem=S["x%d" % rank],
-        srcs=[T["qx"][:, a:a + NC].bitcast(dt.uint8)],
-        dsts=[T["qx"][:, a:a + NC].bitcast(dt.uint8) for _ in others])], local_sem=S["left"])
-    g.remote_dma_fused([RemoteDMATransfer(
-        dst_ids=ids, dma_engine_mask=mask_of(off), remote_sem=S["x%d" % rank],
-        srcs=[T["sx"][:, a:a + NC]], dsts=[T["sx"][:, a:a + NC] for _ in others])], local_sem=S["left"])
+    for group in ([order[3]], [order[2], order[1]]):
+        ids = [dest(T.cores[c], core, topo) for c in group]
+        g.remote_dma_fused([RemoteDMATransfer(
+            dst_ids=ids, dma_engine_mask=mask_of(off), remote_sem=S["x%d" % rank],
+            srcs=[cols("qx", rank).bitcast(dt.uint8)],
+            dsts=[cols("qx", rank).bitcast(dt.uint8) for _ in ids])], local_sem=S["left"])
+        g.remote_dma_fused([RemoteDMATransfer(
+            dst_ids=ids, dma_engine_mask=mask_of(off), remote_sem=S["x%d" % rank],
+            srcs=[cols("sx", rank)], dsts=[cols("sx", rank) for _ in ids])], local_sem=S["left"])
     g.wait_ge(S["qdw"], 3)
     b = rank * WCOLS
     g.remote_dma_fused([RemoteDMATransfer(
@@ -215,48 +233,56 @@ def rank_core(g, core, rank, T, topo):
         srcs=[T["sw"][:, b + k * NEARW:b + k * NEARW + NEARW]],
         dsts=[T["rs"][:, 0:NEARW]]) for k, d in enumerate(near)], local_sem=S["left"])
     half = len(off) // 2
-    for k in (1, 2, 3):
+    for k in (1, 2):
         theirs = helpers_of(T.cores[order[k]], topo)[0]
         g.wait_ge(S["out%d" % k], 2)
         g.remote_dma_fused([RemoteDMATransfer(
             dst_ids=[dest(theirs[i], core, topo)], dma_engine_mask=mask_of(off[half * i:half * i + half]), remote_sem=S["sa%d" % k],
-            srcs=[cols("part", 2 * k + i)], dsts=[cols("land", rank)]) for i in (0, 1)], local_sem=S["sleft"])
-    g.wait_ge(S["left"], 2 * len(off) + 2 * NFAR + 4 * NNEAR)
+            srcs=[cols("part", 2 * k + i)], dsts=[cols("land", k)]) for i in (0, 1)], local_sem=S["sleft"])
+    theirs = helpers_of(T.cores[order[3]], topo)[0][1]
+    g.wait_ge(S["out3"], 2)
+    rid, pid = topo.addr(theirs, core)
+    g.remote_dma(T["land"][:, 3 * NC + CUT:4 * NC], T["part"][:, 3 * 256 + STRAIGHT:4 * 256], S["sa3"], S["sleft"],
+                 pid, rid, mask_of(off))
+    rid, pid = topo.addr(T.cores[order[3]], core)
+    g.remote_dma(T["straight"][:, 0:STRAIGHT], T["part"][:, 3 * 256:3 * 256 + STRAIGHT], S["sstr"], S["sleft"],
+                 pid, rid, mask_of(off))
+    g.wait_ge(S["left"], 4 * len(off) + 2 * NFAR + 4 * NNEAR)
 
     g.tensor.wait_ge(S["qd1"], 2)
     g.tensor.wait_ge(S["qdx"], 1)
     z_mm(0)
     g.tensor.wait_ge(S["qd2"], 2)
     p_mm(0)
-    xs = 2 * len(off)
-    for k in (1, 2):
-        g.tensor.wait_ge(S["x%d" % order[k]], xs)
-        z_mm(k)
+    z_mm(1)
     p_mm(1)
-    g.tensor.wait_ge(S["x%d" % order[3]], xs)
+    z_mm(2)
     z_mm(3)
     p_mm(2)
     p_mm(3)
-    for k in (0, 1, 2):
-        t_scalar(k)
-        t_vector(k)
-    p_scalar(1)
-    p_vector(1)
-    t_scalar(3)
-    t_vector(3)
-    for k in (2, 3):
-        p_scalar(k)
-        p_vector(k)
+    make_t(0)
+    make_t(1)
+    take_p(1)
+    make_t(2)
+    make_t(3)
+    take_p(2)
+    take_p(3)
 
-    for i in (0, 1):
-        if i == 0:
-            g.vector.wait_ge(S["pa0"], 1)
-            g.vector.wait_ge(S["pb0"], 1)
-        g.vector.wait_ge(S["f%d" % i], len(off))
-        g.vector.tensor_tensor(cols("sums", i), bank(i), cols("fold", i), AluOpType.add).then_inc(S["h%d" % i], 1)
+    g.vector.wait_ge(S["pa0"], 1)
+    g.vector.wait_ge(S["pb0"], 1)
+    g.vector.wait_ge(S["sstr"], len(off))
+    add(T["pre"][:, 0:NC], bank(0), T["straight"][:, 0:NC], "pre0")
+    add(T["pre"][:, NC:STRAIGHT], bank(1, 0, CUT), T["straight"][:, NC:STRAIGHT], "pre0")
+    g.vector.wait_ge(S["pre0"], 2)
+    g.vector.wait_ge(S["f0"], len(off))
+    add(T["sums"][:, 0:NC], T["pre"][:, 0:NC], T["fold"][:, 0:NC], "h0")
+    g.vector.wait_ge(S["f1"], len(off))
+    add(T["sums"][:, NC:STRAIGHT], T["pre"][:, NC:STRAIGHT], T["fold"][:, NC:STRAIGHT], "h1")
+    g.vector.wait_ge(S["f2"], len(off))
+    add(T["sums"][:, STRAIGHT:256], bank(1, CUT, NC), T["fold"][:, STRAIGHT:256], "h1")
     g.scalar.wait_ge(S["h0"], 1)
     relus("scalar", cols("sums", 0), "hh", 0, 0, C2, "ha")
-    g.vector.wait_ge(S["h1"], 1)
+    g.vector.wait_ge(S["h1"], 2)
     relus("vector", cols("sums", 1), "hh", 0, 1, C2, "ha")
     g.vector.wait_ge(S["ha"], 4)
     g.vector.quantize_mx(cols("qh", 0), cols("sh", 0), T["hh"][:, 0:512]).then_inc(S["hq"], 1)
@@ -284,7 +310,7 @@ def rank_core(g, core, rank, T, topo):
     g.vector.wait_ge(S["ydone"], 1)
     g.vector.tensor_copy(cols("yy", 0), bank(0)).then_inc(S["yc"], 1)
 
-    g.sync.wait_ge(S["sleft"], 3 * len(off))
+    g.sync.wait_ge(S["sleft"], 4 * len(off))
     for k in range(N):
         g.sync.wait_ge(S["act%d" % k], 4)
         g.sync.dma_start(T["t"][order[k]], cols("tt", order[k], 512)).then_inc(S["stored"], 16)

from concourse.bass import DstId, RemoteDMATransfer
from concourse.mybir import dt, AluOpType, ActivationFunctionType

N = 4
NC = 128
WCOLS = 3 * 128
NNEAR, NFAR = 2, 4
FARW, NEARW = WCOLS // NFAR, WCOLS // NNEAR
STRAIGHT = 200
CUT = STRAIGHT - NC
C1, C2 = 0.031, 0.0155
CODES = "float8_e4m3fn_x4"

SCRATCH = {
    "bx": ("sbuf", [128, 512], "bfloat16"),
    "bw1": ("sbuf", [128, 1024], "bfloat16"),
    "bw2": ("sbuf", [128, 1024], "bfloat16"),
    "bw3": ("sbuf", [128, 1024], "bfloat16"),
    "bw4": ("sbuf", [128, 512], "bfloat16"),
    "qx": ("sbuf", [128, N * NC], CODES),
    "sx": ("sbuf", [128, N * NC], "uint8"),
    "qw1": ("sbuf", [128, 256], CODES),
    "sw1": ("sbuf", [128, 256], "uint8"),
    "qw2": ("sbuf", [128, 256], CODES),
    "sw2": ("sbuf", [128, 256], "uint8"),
    "qw": ("sbuf", [128, N * WCOLS], CODES),
    "sw": ("sbuf", [128, N * WCOLS], "uint8"),
    "rq": ("sbuf", [128, FARW], CODES),
    "rs": ("sbuf", [128, NEARW], "uint8"),
    "tt": ("sbuf", [128, N * 512], "bfloat16"),
    "qt": ("sbuf", [128, N * NC], CODES),
    "st": ("sbuf", [128, N * NC], "uint8"),
    "part": ("sbuf", [128, N * 256], "float32"),
    "land": ("sbuf", [128, N * NC], "float32"),
    "two": ("sbuf", [128, NC], "float32"),
    "three": ("sbuf", [128, NC - CUT], "float32"),
    "straight": ("sbuf", [128, STRAIGHT], "float32"),
    "fold": ("sbuf", [128, 256], "float32"),
    "pre": ("sbuf", [128, STRAIGHT], "float32"),
    "sums": ("sbuf", [128, 256], "float32"),
    "hh": ("sbuf", [128, 512], "bfloat16"),
    "qh": ("sbuf", [128, NC], CODES),
    "sh": ("sbuf", [128, NC], "uint8"),
    "uu": ("sbuf", [128, N * 512], "bfloat16"),
    "qu": ("sbuf", [128, N * NC], CODES),
    "su": ("sbuf", [128, N * NC], "uint8"),
    "yy": ("sbuf", [128, NC], "float32"),
    "ps": ("psum", [128, 4096], "float32"),
}
SEMAPHORES = (["xissued", "lx", "lw1", "lw2", "lw3", "lw4", "qdx", "qdw", "qd1", "qd2", "stored",
               "wgot", "warr", "sa1", "sa2", "sa3", "hv2", "hv3", "f0", "f1", "f2", "sstr", "left", "sleft",
               "pre0", "h0", "h1", "ha", "hq", "ydone", "yc"]
              + ["x%d" % k for k in range(N)]
              + [s + str(k) for k in range(N) for s in ("za", "zb", "act", "tq", "pa", "pb", "out", "va", "vb", "uact", "uq")])


def engines(mask):
    return [e for e in range(mask.bit_length()) if mask >> e & 1]


def mask_of(es):
    return sum(1 << e for e in es)


def chip_of(c, topo):
    return topo.host(c), topo.chip(c)


def helpers_of(rc, topo):
    mine = [d for d in range(256) if d != rc and chip_of(d, topo) == chip_of(rc, topo)]
    near = [d for d in mine if topo.die(d) == topo.die(rc)]
    far = [d for d in mine if topo.die(d) != topo.die(rc)]
    return near[:NNEAR], far[:NFAR]


def dest(dst, src, topo):
    rid, pid = topo.addr(dst, src)
    return DstId(rid=rid, pnc=pid)


def rank_program(g, core, T, topo):
    rank = T.rank_of(core)
    if rank is not None:
        rank_core(g, core, rank, T, topo)
        return
    for r in range(N):
        near, far = helpers_of(T.cores[r], topo)
        if core in near:
            near_core(g, core, r, near.index(core), T, topo)
        if core in far:
            far_core(g, core, r, far.index(core), T, topo)


def far_core(g, core, r, k, T, topo):
    S = T.sem
    others = [T.cores[(r + j) % N] for j in range(1, N)]
    off = engines(topo.mask(core, others[0]))
    a = r * WCOLS + k * FARW
    g.wait_ge(S["wgot"], 2)
    g.remote_dma_fused([RemoteDMATransfer(
        dst_ids=[dest(d, core, topo) for d in others], dma_engine_mask=mask_of(off), remote_sem=S["warr"],
        srcs=[T["rq"][:, 0:FARW].bitcast(dt.uint8)],
        dsts=[T["qw"][:, a:a + FARW].bitcast(dt.uint8) for _ in others])], local_sem=S["left"])
    g.wait_ge(S["left"], len(off))


def near_core(g, core, r, k, T, topo):
    S = T.sem
    others = [T.cores[(r + j) % N] for j in range(1, N)]
    off = engines(topo.mask(core, others[0]))
    a = r * WCOLS + k * NEARW
    g.wait_ge(S["wgot"], 4)
    g.remote_dma_fused([RemoteDMATransfer(
        dst_ids=[dest(d, core, topo) for d in others], dma_engine_mask=mask_of(off), remote_sem=S["warr"],
        srcs=[T["rs"][:, 0:NEARW]],
        dsts=[T["sw"][:, a:a + NEARW] for _ in others])], local_sem=S["left"])

    def land(j, lo):
        return T["land"][:, j * NC + lo:j * NC + NC]

    for j in (1, 2):
        g.vector.wait_ge(S["sa%d" % j], len(off) // 2)
    g.vector.tensor_tensor(T["two"][:, 0:NC], land(1, 0), land(2, 0), AluOpType.add).then_inc(S["hv2"], 1)
    rid, pid = topo.addr(T.cores[r], core)
    w = CUT if k else NC
    g.wait_ge(S["hv2"], 1)
    g.remote_dma(T["fold"][:, k * NC:k * NC + w], T["two"][:, 0:w], S["f%d" % k], S["left"], pid, rid, mask_of(off))
    n = 2 * len(off)
    if k:
        g.vector.wait_ge(S["hv2"], 1)
        g.vector.wait_ge(S["sa3"], len(off))
        g.vector.tensor_tensor(T["three"][:, 0:NC - CUT], T["two"][:, CUT:NC], land(3, CUT), AluOpType.add).then_inc(S["hv3"], 1)
        g.wait_ge(S["hv3"], 1)
        g.remote_dma(T["fold"][:, STRAIGHT:256], T["three"][:, 0:NC - CUT], S["f2"], S["left"], pid, rid, mask_of(off))
        n += len(off)
    g.wait_ge(S["left"], n)


def rank_core(g, core, rank, T, topo):
    S = T.sem
    order = [(rank + k) % N for k in range(N)]
    near, far = helpers_of(core, topo)
    off = engines(topo.mask(core, T.cores[order[1]]))
    chip_only = [e for e in engines(topo.mask(core, near[0])) if e not in off]
    relu, copy = ActivationFunctionType.Relu, ActivationFunctionType.Copy

    def bank(b, lo=0, hi=NC):
        return T["ps"][:, 512 * b + lo:512 * b + hi]

    def cols(name, i, w=NC):
        return T[name][:, i * w:i * w + w]

    def load(q, name):
        q.dma_start(T["b" + name][:], T[name][:]).then_inc(S["l" + name], 16)

    load(g.sync, "x")
    g.sync.sem_inc(S["xissued"], 1)
    load(g.sync, "w3")
    load(g.sync, "w4")
    g.scalar.wait_ge(S["xissued"], 1)
    load(g.scalar, "w1")
    load(g.scalar, "w2")

    def relus(eng, src, buf, slot, i, c, sem):
        for s in (0, 1):
            out = T[buf][:, 512 * slot + 2 * i + s:512 * slot + 512:4]
            f = -c if s else c
            if eng == "scalar":
                g.scalar.activation(out, src, relu, scale=f).then_inc(S[sem], 1)
            else:
                g.vector.tensor_scalar(out, src, f, 0.0, AluOpType.mult, AluOpType.max).then_inc(S[sem], 1)

    def mm(b, w, sw, wi, m, sm, mi, start=True, stop=True):
        return g.tensor.matmul_mx(bank(b), cols(w, wi), cols(sw, wi), cols(m, mi), cols(sm, mi), start, stop)

    def z_mm(k):
        if k > 0:
            g.tensor.wait_ge(S["x%d" % order[k]], 2 * len(off))
        mm(2 * k, "qw1", "sw1", 0, "qx", "sx", order[k]).then_inc(S["za%d" % k], 1)
        mm(2 * k + 1, "qw1", "sw1", 1, "qx", "sx", order[k]).then_inc(S["zb%d" % k], 1)

    def p_mm(k):
        g.tensor.wait_ge(S["tq%d" % k], 1)
        mm(2 * k, "qw2", "sw2", 0, "qt", "st", order[k]).then_inc(S["pa%d" % k], 1)
        mm(2 * k + 1, "qw2", "sw2", 1, "qt", "st", order[k]).then_inc(S["pb%d" % k], 1)

    def make_t(k):
        g.scalar.wait_ge(S["za%d" % k], 1)
        relus("scalar", bank(2 * k), "tt", order[k], 0, C1, "act%d" % k)
        g.vector.wait_ge(S["zb%d" % k], 1)
        relus("vector", bank(2 * k + 1), "tt", order[k], 1, C1, "act%d" % k)
        g.vector.wait_ge(S["act%d" % k], 4)
        g.vector.quantize_mx(cols("qt", order[k]), cols("st", order[k]), cols("tt", order[k], 512)).then_inc(S["tq%d" % k], 1)

    def take_p(k):
        g.scalar.wait_ge(S["pa%d" % k], 1)
        g.scalar.activation(cols("part", 2 * k), bank(2 * k), copy).then_inc(S["out%d" % k], 1)
        g.vector.wait_ge(S["pb%d" % k], 1)
        g.vector.tensor_copy(cols("part", 2 * k + 1), bank(2 * k + 1)).then_inc(S["out%d" % k], 1)

    def add(out, a, b, sem):
        g.vector.tensor_tensor(out, a, b, AluOpType.add).then_inc(S[sem], 1)

    g.vector.wait_ge(S["lx"], 16)
    g.vector.quantize_mx(cols("qx", rank), cols("sx", rank), T["bx"][:, 0:512]).then_inc(S["qdx"], 1)
    for name, i, j in (("w3", 0, 0), ("w3", 1, 1), ("w4", 0, 2)):
        if i == 0:
            g.vector.wait_ge(S["l" + name], 16)
        g.vector.quantize_mx(cols("qw", 3 * rank + j), cols("sw", 3 * rank + j), cols("b" + name, i, 512)).then_inc(S["qdw"], 1)
    for name in ("1", "2"):
        g.vector.wait_ge(S["lw" + name], 16)
        for i in (0, 1):
            g.vector.quantize_mx(cols("qw" + name, i), cols("sw" + name, i), cols("bw" + name, i, 512)).then_inc(S["qd" + name], 1)

    g.wait_ge(S["qdx"], 1)
    for group in ([order[3]], [order[2], order[1]]):
        ids = [dest(T.cores[c], core, topo) for c in group]
        g.remote_dma_fused([RemoteDMATransfer(
            dst_ids=ids, dma_engine_mask=mask_of(off), remote_sem=S["x%d" % rank],
            srcs=[cols("qx", rank).bitcast(dt.uint8)],
            dsts=[cols("qx", rank).bitcast(dt.uint8) for _ in ids])], local_sem=S["left"])
        g.remote_dma_fused([RemoteDMATransfer(
            dst_ids=ids, dma_engine_mask=mask_of(off), remote_sem=S["x%d" % rank],
            srcs=[cols("sx", rank)], dsts=[cols("sx", rank) for _ in ids])], local_sem=S["left"])
    g.wait_ge(S["qdw"], 3)
    b = rank * WCOLS
    g.remote_dma_fused([RemoteDMATransfer(
        dst_ids=[dest(d, core, topo)], dma_engine_mask=mask_of(chip_only[2 * k:2 * k + 2]), remote_sem=S["wgot"],
        srcs=[T["qw"][:, b + k * FARW:b + k * FARW + FARW].bitcast(dt.uint8)],
        dsts=[T["rq"][:, 0:FARW].bitcast(dt.uint8)]) for k, d in enumerate(far)], local_sem=S["left"])
    g.remote_dma_fused([RemoteDMATransfer(
        dst_ids=[dest(d, core, topo)], dma_engine_mask=mask_of(chip_only[4 * k:4 * k + 4]), remote_sem=S["wgot"],
        srcs=[T["sw"][:, b + k * NEARW:b + k * NEARW + NEARW]],
        dsts=[T["rs"][:, 0:NEARW]]) for k, d in enumerate(near)], local_sem=S["left"])
    half = len(off) // 2
    for k in (1, 2):
        theirs = helpers_of(T.cores[order[k]], topo)[0]
        g.wait_ge(S["out%d" % k], 2)
        g.remote_dma_fused([RemoteDMATransfer(
            dst_ids=[dest(theirs[i], core, topo)], dma_engine_mask=mask_of(off[half * i:half * i + half]), remote_sem=S["sa%d" % k],
            srcs=[cols("part", 2 * k + i)], dsts=[cols("land", k)]) for i in (0, 1)], local_sem=S["sleft"])
    theirs = helpers_of(T.cores[order[3]], topo)[0][1]
    g.wait_ge(S["out3"], 2)
    rid, pid = topo.addr(theirs, core)
    g.remote_dma(T["land"][:, 3 * NC + CUT:4 * NC], T["part"][:, 3 * 256 + STRAIGHT:4 * 256], S["sa3"], S["sleft"],
                 pid, rid, mask_of(off))
    rid, pid = topo.addr(T.cores[order[3]], core)
    g.remote_dma(T["straight"][:, 0:STRAIGHT], T["part"][:, 3 * 256:3 * 256 + STRAIGHT], S["sstr"], S["sleft"],
                 pid, rid, mask_of(off))
    g.wait_ge(S["left"], 4 * len(off) + 2 * NFAR + 4 * NNEAR)

    g.tensor.wait_ge(S["qd1"], 2)
    g.tensor.wait_ge(S["qdx"], 1)
    z_mm(0)
    g.tensor.wait_ge(S["qd2"], 2)
    p_mm(0)
    z_mm(1)
    p_mm(1)
    z_mm(2)
    z_mm(3)
    p_mm(2)
    p_mm(3)
    make_t(0)
    make_t(1)
    take_p(1)
    make_t(2)
    make_t(3)
    take_p(2)
    take_p(3)

    g.vector.wait_ge(S["pa0"], 1)
    g.vector.wait_ge(S["pb0"], 1)
    g.vector.wait_ge(S["sstr"], len(off))
    add(T["pre"][:, 0:NC], bank(0), T["straight"][:, 0:NC], "pre0")
    add(T["pre"][:, NC:STRAIGHT], bank(1, 0, CUT), T["straight"][:, NC:STRAIGHT], "pre0")
    g.vector.wait_ge(S["pre0"], 2)
    g.vector.wait_ge(S["f0"], len(off))
    add(T["sums"][:, 0:NC], T["pre"][:, 0:NC], T["fold"][:, 0:NC], "h0")
    g.vector.wait_ge(S["f1"], len(off))
    add(T["sums"][:, NC:STRAIGHT], T["pre"][:, NC:STRAIGHT], T["fold"][:, NC:STRAIGHT], "h1")
    g.vector.wait_ge(S["f2"], len(off))
    add(T["sums"][:, STRAIGHT:256], bank(1, CUT, NC), T["fold"][:, STRAIGHT:256], "h1")
    g.scalar.wait_ge(S["h0"], 1)
    relus("scalar", cols("sums", 0), "hh", 0, 0, C2, "ha")
    g.vector.wait_ge(S["h1"], 2)
    relus("vector", cols("sums", 1), "hh", 0, 1, C2, "ha")
    g.vector.wait_ge(S["ha"], 4)
    g.vector.quantize_mx(cols("qh", 0), cols("sh", 0), T["hh"][:, 0:512]).then_inc(S["hq"], 1)

    g.tensor.wait_ge(S["hq"], 1)
    for k in range(N):
        if k == 1:
            g.tensor.wait_ge(S["warr"], 3 * (NNEAR + NFAR) * len(off))
        mm(2 * k, "qw", "sw", 3 * order[k], "qh", "sh", 0).then_inc(S["va%d" % k], 1)
        mm(2 * k + 1, "qw", "sw", 3 * order[k] + 1, "qh", "sh", 0).then_inc(S["vb%d" % k], 1)
    for k in range(N):
        g.scalar.wait_ge(S["va%d" % k], 1)
        relus("scalar", bank(2 * k), "uu", k, 0, C1, "uact%d" % k)
    for k in range(N + 1):
        if k < N:
            g.vector.wait_ge(S["vb%d" % k], 1)
            relus("vector", bank(2 * k + 1), "uu", k, 1, C1, "uact%d" % k)
        if k > 0:
            g.vector.wait_ge(S["uact%d" % (k - 1)], 4)
            g.vector.quantize_mx(cols("qu", k - 1), cols("su", k - 1), cols("uu", k - 1, 512)).then_inc(S["uq%d" % (k - 1)], 1)
    for k in range(N):
        g.tensor.wait_ge(S["uq%d" % k], 1)
        p = mm(0, "qw", "sw", 3 * order[k] + 2, "qu", "su", k, start=k == 0, stop=k == N - 1)
    p.then_inc(S["ydone"], 1)
    g.vector.wait_ge(S["ydone"], 1)
    g.vector.tensor_copy(cols("yy", 0), bank(0)).then_inc(S["yc"], 1)

    g.sync.wait_ge(S["sleft"], 4 * len(off))
    for k in range(N):
        g.sync.wait_ge(S["act%d" % k], 4)
        g.sync.dma_start(T["t"][order[k]], cols("tt", order[k], 512)).then_inc(S["stored"], 16)
    g.sync.wait_ge(S["ha"], 4)
    g.sync.dma_start(T["h"][:], T["hh"][:]).then_inc(S["stored"], 16)
    g.sync.wait_ge(S["yc"], 1)
    g.sync.dma_start(T["y"][:], T["yy"][:]).then_inc(S["stored"], 16)
    g.sync.wait_ge(S["stored"], 16 * (N + 2))
